import numpy as np
import ml_dtypes


def mxq(x, axis, fmt="e4m3"):
    dtype, down = {"e4m3": (ml_dtypes.float8_e4m3fn, 7), "e5m2": (ml_dtypes.float8_e5m2, 14)}[fmt]
    v = np.moveaxis(np.asarray(x, np.float32).astype(ml_dtypes.bfloat16).astype(np.float64), axis, -1)
    blocks = v.reshape(v.shape[:-1] + (-1, 32))
    amax = np.abs(blocks).max(-1, keepdims=True)
    byte = np.maximum(np.where(amax > 0, np.frexp(amax)[1] - 1 + 127, 0) - down, 1)
    scale = np.exp2(byte - 127.0)
    codes = (blocks / scale).astype(np.float32).astype(dtype).astype(np.float64)
    return np.moveaxis((codes * scale).reshape(v.shape), -1, axis)


WIDE = False


def mx_kscale(k):
    if not WIDE:
        return np.ones(k)
    levels = np.array([10, -10, 5, -5, 0])
    if k % 512:
        return np.exp2(np.random.permutation(np.resize(levels, k // 32))).repeat(32)
    a = np.empty((k // 512, 16))
    for p in range(k // 512):
        a[p, :8] = np.random.permutation(np.resize(levels, 8))
        for g in range(8):
            far = levels[np.abs(levels - a[p, g]) >= 10]
            a[p, g + 8] = far[np.random.randint(len(far))]
    return np.exp2(a.ravel()).repeat(32)


def f64(x):
    return np.asarray(x).astype(np.float64)


def striped(idx):
    return np.tile(idx.reshape(-1, 16).T, (8, 1)).astype(np.uint16)


def unstriped(offs):
    return offs[:16].T.reshape(-1).astype(np.int64)


def pack_weight(w):
    k, n = w.shape
    w = f64(np.asarray(w, np.float32).astype(ml_dtypes.bfloat16)).reshape(k // 32, 32, n)
    amax = np.abs(w).max(1)
    byte = np.clip(np.where(amax > 0, np.frexp(amax)[1] - 1 + 127 - 7, 1), 1, 254)
    scaled = (w * np.exp2(127.0 - byte)[:, None, :]).reshape(k, n).astype(np.float32)
    words = np.ascontiguousarray(scaled.reshape(k // 512, 128, 4, n).transpose(0, 1, 3, 2)).astype(ml_dtypes.float8_e4m3fn).view(np.uint8)
    return words, np.ascontiguousarray(byte.astype(np.uint8).reshape(k // 512, 16, n))


def unpack_weight(words, scales):
    g, p, n, _ = words.shape
    vals = np.ascontiguousarray(words).view(ml_dtypes.float8_e4m3fn).astype(np.float64) * np.repeat(np.exp2(scales.astype(np.float64) - 127.0), 8, axis=1)[..., None]
    return vals.transpose(0, 1, 3, 2).reshape(g * 512, n)


def sigmoid(v):
    return 1.0 / (1.0 + np.exp(-np.maximum(v, -700.0)))


K, T, S, J = 1024, 2048, 512, 256


def setup_inputs():
    n = np.random.standard_normal
    s = mx_kscale(K)[:, None]
    packed_xT = pack_weight(n((K, T)) * s)
    packed_eT = pack_weight(n((K, T)) * s)
    return {
        "x_words": packed_xT[0],
        "x_scales": packed_xT[1],
        "e_words": packed_eT[0],
        "e_scales": packed_eT[1],
        "hT": (n((K, J)) / np.sqrt(K) / s).astype(np.float32),
        "gT": (n((K, J)) / np.sqrt(K) / s).astype(np.float32),
        "offs": striped(np.random.permutation(T)[:S]),
    }


def reference(x_words, x_scales, e_words, e_scales, hT, gT, offs):
    hTq = mxq(f64(hT), 0, "e4m3")
    xq = unpack_weight(x_words, x_scales)[:, unstriped(offs)]
    gTq = mxq(f64(gT), 0, "e4m3")
    e_offs = unpack_weight(e_words, e_scales)[:, unstriped(offs)]
    y = hTq.T @ xq + gTq.T @ e_offs
    return sigmoid(y)

@@ -1,0 +1,152 @@
+from contextlib import ExitStack
+
+import concourse.mybir as mybir
+
+K, T, S, J = 1024, 2048, 512, 256
+FLOPS = 2 * 2 * K * J * S
+
+F32 = mybir.dt.float32
+BF16 = mybir.dt.bfloat16
+I32 = mybir.dt.int32
+U32 = mybir.dt.uint32
+U16 = mybir.dt.uint16
+U8 = mybir.dt.uint8
+FP8X4 = mybir.dt.float8_e4m3fn_x4
+SIGMOID = mybir.ActivationFunctionType.Sigmoid
+
+P = 128
+PACK = 4
+K_PASS = P * PACK
+PASSES = K // K_PASS
+HALF = S // 2
+QUADS = 4
+ROWS = 4
+
+
+def tile_picked_zhyb_sig_p_kernel(tc, x_words, x_scales, e_words, e_scales, hT, gT, offs, out):
+    nc = tc.nc
+    with ExitStack() as ctx:
+        keep = ctx.enter_context(tc.tile_pool(name="keep", bufs=1))
+        psum = ctx.enter_context(tc.psum_pool(name="psum", bufs=1))
+
+        offsets = keep.tile([P, S // 16], U16, name="offsets")
+        tables = [(x_words, x_scales, hT), (e_words, e_scales, gT)]
+        steps = [(t, o) for t in range(2) for o in range(PASSES)]
+
+        warm_in = keep.tile([P, 8], F32, name="warm_in")
+        warm_out = keep.tile([P, 8], F32, name="warm_out")
+        nc.vector.memset(warm_in[:], 0.0)
+        nc.scalar.activation(warm_out[:], warm_in[:], SIGMOID)
+
+        words = {}
+        raw = {}
+        for t, o in steps:
+            words[t, o] = keep.tile([P, T], U32, name=f"words{t}{o}")
+            raw[t, o] = keep.tile([P, PACK, J], F32, name=f"raw{t}{o}")
+
+        def load_words(t, o):
+            nc.sync.dma_start(
+                out=words[t, o][:].bitcast(I32),
+                in_=tables[t][0][o].rearrange("p n r -> p (n r)").bitcast(I32),
+            )
+
+        def load_queries(t, o):
+            rows = tables[t][2][o * K_PASS : (o + 1) * K_PASS, :]
+            nc.sync.dma_start(out=raw[t, o][:], in_=rows.rearrange("(p r) j -> p r j", r=PACK))
+
+        load_words(0, 0)
+        nc.sync.dma_start(offsets[:], offs)
+        load_words(0, 1)
+        for t, o in steps:
+            load_queries(t, o)
+        load_words(1, 0)
+        load_words(1, 1)
+
+        def plane_row(t, o):
+            return ROWS * (PASSES * t + o)
+
+        scale_table = []
+        for t in range(2):
+            planes = keep.tile([P, T], U8, name=f"planes{t}")
+            nc.vector.memset(planes[:].bitcast(I32), 0)
+            for q in range(QUADS):
+                first = 32 * q + plane_row(t, 0)
+                nc.gpsimd.dma_start(
+                    out=planes[first : first + PASSES * ROWS, :].bitcast(I32),
+                    in_=tables[t][1][:, ROWS * q : ROWS * (q + 1), :].bitcast(I32),
+                )
+            scale_table.append(planes)
+
+        half_offsets = [offsets[:, h * (HALF // 16) : (h + 1) * (HALF // 16)] for h in range(2)]
+        banks = {}
+        for h in range(2):
+            for m in range(J // P):
+                banks[h, m] = psum.tile([P, HALF], F32, name=f"bank{h}{m}")
+
+        doc_words = {}
+        doc_scales = {}
+        codes = {}
+        scales = {}
+
+        def pick_words(t, o):
+            if (t, o) == steps[-1]:
+                halves = []
+                for h in range(2):
+                    picked = keep.tile([P, HALF], U32, name=f"picked_last{h}", align_bytes=64)
+                    nc.vector.tensor_copy(picked[:], words[t, o][:].indirect(half_offsets[h]))
+                    halves.append(picked[:])
+            else:
+                picked = keep.tile([P, S], U32, name=f"picked{t}{o}", align_bytes=64)
+                nc.vector.tensor_copy(picked[:], words[t, o][:].indirect(offsets[:]))
+                halves = [picked[:, h * HALF : (h + 1) * HALF] for h in range(2)]
+            doc_words[t, o] = halves
+
+        def pick_scales(t):
+            doc_scales[t] = keep.tile([P, S], U8, name=f"doc_scales{t}", align_bytes=64)
+            nc.vector.tensor_copy(doc_scales[t][:], scale_table[t][:].indirect(offsets[:]))
+
+        def quantise(t, o):
+            grouped = keep.tile([P, J, PACK], BF16, name=f"grouped{t}{o}", align_bytes=64)
+            nc.scalar.copy(
+                out=grouped[:].rearrange("p (c i) r -> p c r i", i=4),
+                in_=raw[t, o][:].rearrange("p r (c i) -> p c r i", i=4),
+            )
+            codes[t, o] = keep.tile([P, J], U32, name=f"codes{t}{o}", align_bytes=64)
+            scales[t, o] = keep.tile([P, J], U8, name=f"scales{t}{o}", align_bytes=64)
+            nc.vector.quantize_mx(
+                out=codes[t, o][:].bitcast(FP8X4),
+                scales=scales[t, o][:],
+                in_=grouped[:].rearrange("p j r -> p (j r)"),
+            )
+
+        def multiply(t, o):
+            for h in range(2):
+                for m in range(J // P):
+                    nc.tensor.matmul_mx(
+                        out=banks[h, m][:],
+                        lhsT=codes[t, o][:, m * P : (m + 1) * P].bitcast(FP8X4),
+                        lhsT_scale=scales[t, o][:, m * P : (m + 1) * P],
+                        rhs=doc_words[t, o][h].bitcast(FP8X4),
+                        rhs_scale=doc_scales[t][plane_row(t, o) :, h * HALF : (h + 1) * HALF],
+                        start=(t, o) == steps[0],
+                        stop=(t, o) == steps[-1],
+                    )
+
+        pick_words(0, 0)
+        pick_words(0, 1)
+        pick_scales(0)
+        quantise(0, 0)
+        quantise(0, 1)
+        pick_scales(1)
+        quantise(1, 0)
+        quantise(1, 1)
+        pick_words(1, 0)
+        pick_words(1, 1)
+        for t, o in steps:
+            multiply(t, o)
+
+        for h in range(2):
+            for m in range(J // P):
+                result = keep.tile([P, HALF], F32, name=f"result{h}{m}")
+                nc.scalar.activation(result[:], banks[h, m][:], SIGMOID)
+                nc.sync.dma_start(out=out[m * P : (m + 1) * P, h * HALF : (h + 1) * HALF], in_=result[:])

@@ -41,7 +41,7 @@ def tile_picked_zhyb_sig_p_kernel(tc, x_words, x_scales, e_words, e_scales, hT, 
         words = {}
         raw = {}
         for t, o in steps:
-            words[t, o] = keep.tile([P, T], U32, name=f"words{t}{o}")
+            words[t, o] = keep.tile([P, T], U32, name=f"words{t}{o}", tag=f"words{t}{o}", align_bytes=64)
             raw[t, o] = keep.tile([P, PACK, J], F32, name=f"raw{t}{o}")
 
         def load_words(t, o):
@@ -102,11 +102,11 @@ def tile_picked_zhyb_sig_p_kernel(tc, x_words, x_scales, e_words, e_scales, hT, 
             doc_words[t, o] = halves
 
         def pick_scales(t):
-            doc_scales[t] = keep.tile([P, S], U8, name=f"doc_scales{t}", align_bytes=64)
+            doc_scales[t] = keep.tile([P, S], U8, name=f"doc_scales{t}", tag=["words01", "grouped01"][t], align_bytes=64)
             nc.vector.tensor_copy(doc_scales[t][:], scale_table[t][:].indirect(offsets[:]))
 
         def quantise(t, o):
-            grouped = keep.tile([P, J, PACK], BF16, name=f"grouped{t}{o}", align_bytes=64)
+            grouped = keep.tile([P, J, PACK], BF16, name=f"grouped{t}{o}", tag=f"grouped{t}{o}", align_bytes=64)
             nc.scalar.copy(
                 out=grouped[:].rearrange("p (c i) r -> p c r i", i=4),
                 in_=raw[t, o][:].rearrange("p r (c i) -> p c r i", i=4),

@@ -54,13 +54,11 @@ def tile_picked_zhyb_sig_p_kernel(tc, x_words, x_scales, e_words, e_scales, hT, 
             rows = tables[t][2][o * K_PASS : (o + 1) * K_PASS, :]
             nc.sync.dma_start(out=raw[t, o][:], in_=rows.rearrange("(p r) j -> p r j", r=PACK))
 
-        load_words(0, 0)
-        nc.sync.dma_start(offsets[:], offs)
-        load_words(0, 1)
         for t, o in steps:
             load_queries(t, o)
-        load_words(1, 0)
-        load_words(1, 1)
+        nc.sync.dma_start(offsets[:], offs)
+        for t, o in steps:
+            load_words(t, o)
 
         def plane_row(t, o):
             return ROWS * (PASSES * t + o)
@@ -102,7 +100,7 @@ def tile_picked_zhyb_sig_p_kernel(tc, x_words, x_scales, e_words, e_scales, hT, 
             doc_words[t, o] = halves
 
         def pick_scales(t):
-            doc_scales[t] = keep.tile([P, S], U8, name=f"doc_scales{t}", tag=["words01", "grouped01"][t], align_bytes=64)
+            doc_scales[t] = keep.tile([P, S], U8, name=f"doc_scales{t}", tag=["grouped10", "words01"][t], align_bytes=64)
             nc.vector.tensor_copy(doc_scales[t][:], scale_table[t][:].indirect(offsets[:]))
 
         def quantise(t, o):
@@ -132,14 +130,14 @@ def tile_picked_zhyb_sig_p_kernel(tc, x_words, x_scales, e_words, e_scales, hT, 
                         stop=(t, o) == steps[-1],
                     )
 
-        pick_words(0, 0)
-        pick_words(0, 1)
-        pick_scales(0)
         quantise(0, 0)
         quantise(0, 1)
-        pick_scales(1)
         quantise(1, 0)
+        pick_scales(0)
         quantise(1, 1)
+        pick_words(0, 0)
+        pick_words(0, 1)
+        pick_scales(1)
         pick_words(1, 0)
         pick_words(1, 1)
         for t, o in steps:

@@ -18,9 +18,11 @@ P = 128
 PACK = 4
 K_PASS = P * PACK
 PASSES = K // K_PASS
+TABLES = 2
 HALF = S // 2
-QUADS = 4
+QUAD = 32
 ROWS = 4
+SPREAD = 8
 
 
 def tile_picked_zhyb_sig_p_kernel(tc, x_words, x_scales, e_words, e_scales, hT, gT, offs, out):
@@ -31,49 +33,38 @@ def tile_picked_zhyb_sig_p_kernel(tc, x_words, x_scales, e_words, e_scales, hT, 
 
         offsets = keep.tile([P, S // 16], U16, name="offsets")
         tables = [(x_words, x_scales, hT), (e_words, e_scales, gT)]
-        steps = [(t, o) for t in range(2) for o in range(PASSES)]
+        steps = [(t, o) for o in range(PASSES) for t in range(TABLES)]
 
-        warm_in = keep.tile([P, 8], F32, name="warm_in")
-        warm_out = keep.tile([P, 8], F32, name="warm_out")
-        nc.vector.memset(warm_in[:], 0.0)
-        nc.scalar.activation(warm_out[:], warm_in[:], SIGMOID)
+        nc.sync.dma_start(offsets[:], offs)
+
+        scale_rows = []
+        for t in range(TABLES):
+            rows = keep.tile([P, T], U8, name=f"scale_rows{t}")
+            nc.vector.memset(rows[:].bitcast(I32), 0)
+            for o in range(PASSES):
+                nc.sync.dma_start(
+                    out=rows[ROWS * o : P : SPREAD, :].bitcast(I32),
+                    in_=tables[t][1][o].bitcast(I32),
+                )
+            scale_rows.append(rows)
+
+        raw = []
+        for t in range(TABLES):
+            queries = keep.tile([P, PASSES, PACK * J], F32, name=f"raw{t}", tag=f"raw{t}", align_bytes=64)
+            nc.sync.dma_start(out=queries[:], in_=tables[t][2].rearrange("(o p r) j -> p o (r j)", o=PASSES, r=PACK))
+            raw.append(queries)
 
         words = {}
-        raw = {}
         for t, o in steps:
-            words[t, o] = keep.tile([P, T], U32, name=f"words{t}{o}", tag=f"words{t}{o}", align_bytes=64)
-            raw[t, o] = keep.tile([P, PACK, J], F32, name=f"raw{t}{o}")
-
-        def load_words(t, o):
+            words[t, o] = keep.tile([P, T], U32, name=f"words{t}{o}", align_bytes=64)
             nc.sync.dma_start(
                 out=words[t, o][:].bitcast(I32),
                 in_=tables[t][0][o].rearrange("p n r -> p (n r)").bitcast(I32),
             )
 
-        def load_queries(t, o):
-            rows = tables[t][2][o * K_PASS : (o + 1) * K_PASS, :]
-            nc.sync.dma_start(out=raw[t, o][:], in_=rows.rearrange("(p r) j -> p r j", r=PACK))
-
-        for t, o in steps:
-            load_queries(t, o)
-        nc.sync.dma_start(offsets[:], offs)
-        for t, o in steps:
-            load_words(t, o)
-
-        def plane_row(t, o):
-            return ROWS * (PASSES * t + o)
-
-        scale_table = []
-        for t in range(2):
-            planes = keep.tile([P, T], U8, name=f"planes{t}")
-            nc.vector.memset(planes[:].bitcast(I32), 0)
-            for q in range(QUADS):
-                first = 32 * q + plane_row(t, 0)
-                nc.gpsimd.dma_start(
-                    out=planes[first : first + PASSES * ROWS, :].bitcast(I32),
-                    in_=tables[t][1][:, ROWS * q : ROWS * (q + 1), :].bitcast(I32),
-                )
-            scale_table.append(planes)
+        picked_scales = keep.tile([P, TABLES * S], U8, name="picked_scales", align_bytes=64)
+        for t in range(TABLES):
+            nc.vector.tensor_copy(picked_scales[:, t * S : (t + 1) * S], scale_rows[t][:].indirect(offsets[:]))
 
         half_offsets = [offsets[:, h * (HALF // 16) : (h + 1) * (HALF // 16)] for h in range(2)]
         banks = {}
@@ -82,7 +73,6 @@ def tile_picked_zhyb_sig_p_kernel(tc, x_words, x_scales, e_words, e_scales, hT, 
                 banks[h, m] = psum.tile([P, HALF], F32, name=f"bank{h}{m}")
 
         doc_words = {}
-        doc_scales = {}
         codes = {}
         scales = {}
 
@@ -99,15 +89,11 @@ def tile_picked_zhyb_sig_p_kernel(tc, x_words, x_scales, e_words, e_scales, hT, 
                 halves = [picked[:, h * HALF : (h + 1) * HALF] for h in range(2)]
             doc_words[t, o] = halves
 
-        def pick_scales(t):
-            doc_scales[t] = keep.tile([P, S], U8, name=f"doc_scales{t}", tag=["grouped10", "words01"][t], align_bytes=64)
-            nc.vector.tensor_copy(doc_scales[t][:], scale_table[t][:].indirect(offsets[:]))
-
         def quantise(t, o):
             grouped = keep.tile([P, J, PACK], BF16, name=f"grouped{t}{o}", tag=f"grouped{t}{o}", align_bytes=64)
             nc.scalar.copy(
                 out=grouped[:].rearrange("p (c i) r -> p c r i", i=4),
-                in_=raw[t, o][:].rearrange("p r (c i) -> p c r i", i=4),
+                in_=raw[t][:, o, :].rearrange("p (r c i) -> p c r i", r=PACK, i=4),
             )
             codes[t, o] = keep.tile([P, J], U32, name=f"codes{t}{o}", align_bytes=64)
             scales[t, o] = keep.tile([P, J], U8, name=f"scales{t}{o}", align_bytes=64)
@@ -125,21 +111,26 @@ def tile_picked_zhyb_sig_p_kernel(tc, x_words, x_scales, e_words, e_scales, hT, 
                         lhsT=codes[t, o][:, m * P : (m + 1) * P].bitcast(FP8X4),
                         lhsT_scale=scales[t, o][:, m * P : (m + 1) * P],
                         rhs=doc_words[t, o][h].bitcast(FP8X4),
-                        rhs_scale=doc_scales[t][plane_row(t, o) :, h * HALF : (h + 1) * HALF],
+                        rhs_scale=doc_scales[o][ROWS * o :, t * S + h * HALF : t * S + (h + 1) * HALF],
                         start=(t, o) == steps[0],
                         stop=(t, o) == steps[-1],
                     )
 
-        quantise(0, 0)
-        quantise(0, 1)
-        quantise(1, 0)
-        pick_scales(0)
-        quantise(1, 1)
-        pick_words(0, 0)
-        pick_words(0, 1)
-        pick_scales(1)
-        pick_words(1, 0)
-        pick_words(1, 1)
+        for t in range(TABLES):
+            for o in range(PASSES):
+                quantise(t, o)
+        doc_scales = []
+        for o in range(PASSES):
+            planes = keep.tile([P, TABLES * S], U8, name=f"doc_scales{o}", tag=["raw1", "grouped11"][o], align_bytes=64)
+            nc.vector.tensor_copy(planes[:].bitcast(I32), picked_scales[:].bitcast(I32))
+            doc_scales.append(planes)
+            for i in range(1, ROWS):
+                nc.scalar.dma_start(
+                    out=doc_scales[o][ROWS * o + i : P : QUAD, :].bitcast(I32),
+                    in_=picked_scales[ROWS * o + SPREAD * i : P : QUAD, :].bitcast(I32),
+                )
+        for t, o in steps:
+            pick_words(t, o)
         for t, o in steps:
             multiply(t, o)
 

@@ -48,23 +48,38 @@ def tile_picked_zhyb_sig_p_kernel(tc, x_words, x_scales, e_words, e_scales, hT, 
                 )
             scale_rows.append(rows)
 
-        raw = []
-        for t in range(TABLES):
-            queries = keep.tile([P, PASSES, PACK * J], F32, name=f"raw{t}", tag=f"raw{t}", align_bytes=64)
-            nc.sync.dma_start(out=queries[:], in_=tables[t][2].rearrange("(o p r) j -> p o (r j)", o=PASSES, r=PACK))
-            raw.append(queries)
+        raw = {}
+        for t, o in steps:
+            raw[t, o] = keep.tile([P, PACK * J], F32, name=f"raw{t}{o}")
+            rows = tables[t][2][o * K_PASS : (o + 1) * K_PASS, :]
+            nc.sync.dma_start(out=raw[t, o][:], in_=rows.rearrange("(p r) j -> p (r j)", r=PACK))
 
         words = {}
-        for t, o in steps:
-            words[t, o] = keep.tile([P, T], U32, name=f"words{t}{o}", align_bytes=64)
+
+        def load_words(t, o, tag):
+            words[t, o] = keep.tile([P, T], U32, name=f"words{t}{o}", tag=tag, align_bytes=64)
             nc.sync.dma_start(
                 out=words[t, o][:].bitcast(I32),
                 in_=tables[t][0][o].rearrange("p n r -> p (n r)").bitcast(I32),
             )
 
+        for t in range(TABLES):
+            load_words(t, 0, f"words{t}0")
+
         picked_scales = keep.tile([P, TABLES * S], U8, name="picked_scales", align_bytes=64)
         for t in range(TABLES):
             nc.vector.tensor_copy(picked_scales[:, t * S : (t + 1) * S], scale_rows[t][:].indirect(offsets[:]))
+
+        doc_scales = []
+        for o in range(PASSES):
+            planes = keep.tile([P, TABLES * S], U8, name=f"doc_scales{o}", align_bytes=64)
+            nc.vector.tensor_copy(planes[:].bitcast(I32), picked_scales[:].bitcast(I32))
+            doc_scales.append(planes)
+            for i in range(1, ROWS):
+                nc.sync.dma_start(
+                    out=planes[ROWS * o + i : P : QUAD, :].bitcast(I32),
+                    in_=picked_scales[ROWS * o + SPREAD * i : P : QUAD, :].bitcast(I32),
+                )
 
         half_offsets = [offsets[:, h * (HALF // 16) : (h + 1) * (HALF // 16)] for h in range(2)]
         banks = {}
@@ -93,7 +108,7 @@ def tile_picked_zhyb_sig_p_kernel(tc, x_words, x_scales, e_words, e_scales, hT, 
             grouped = keep.tile([P, J, PACK], BF16, name=f"grouped{t}{o}", tag=f"grouped{t}{o}", align_bytes=64)
             nc.scalar.copy(
                 out=grouped[:].rearrange("p (c i) r -> p c r i", i=4),
-                in_=raw[t][:, o, :].rearrange("p (r c i) -> p c r i", r=PACK, i=4),
+                in_=raw[t, o][:].rearrange("p (r c i) -> p c r i", r=PACK, i=4),
             )
             codes[t, o] = keep.tile([P, J], U32, name=f"codes{t}{o}", align_bytes=64)
             scales[t, o] = keep.tile([P, J], U8, name=f"scales{t}{o}", align_bytes=64)
@@ -116,19 +131,10 @@ def tile_picked_zhyb_sig_p_kernel(tc, x_words, x_scales, e_words, e_scales, hT, 
                         stop=(t, o) == steps[-1],
                     )
 
+        for t, o in steps:
+            quantise(t, o)
         for t in range(TABLES):
-            for o in range(PASSES):
-                quantise(t, o)
-        doc_scales = []
-        for o in range(PASSES):
-            planes = keep.tile([P, TABLES * S], U8, name=f"doc_scales{o}", tag=["raw1", "grouped11"][o], align_bytes=64)
-            nc.vector.tensor_copy(planes[:].bitcast(I32), picked_scales[:].bitcast(I32))
-            doc_scales.append(planes)
-            for i in range(1, ROWS):
-                nc.scalar.dma_start(
-                    out=doc_scales[o][ROWS * o + i : P : QUAD, :].bitcast(I32),
-                    in_=picked_scales[ROWS * o + SPREAD * i : P : QUAD, :].bitcast(I32),
-                )
+            load_words(t, 1, ["grouped10", "grouped01"][t])
         for t, o in steps:
             pick_words(t, o)
         for t, o in steps:

@@ -35,10 +35,18 @@ def tile_picked_zhyb_sig_p_kernel(tc, x_words, x_scales, e_words, e_scales, hT, 
         tables = [(x_words, x_scales, hT), (e_words, e_scales, gT)]
         steps = [(t, o) for o in range(PASSES) for t in range(TABLES)]
 
-        nc.sync.dma_start(offsets[:], offs)
+        raw = {}
+
+        def load_queries(t, o):
+            raw[t, o] = keep.tile([P, PACK * J], F32, name=f"raw{t}{o}")
+            rows = tables[t][2][o * K_PASS : (o + 1) * K_PASS, :]
+            nc.sync.dma_start(out=raw[t, o][:], in_=rows.rearrange("(p r) j -> p (r j)", r=PACK))
 
         scale_rows = []
         for t in range(TABLES):
+            load_queries(t, 0)
+            if t == 0:
+                nc.sync.dma_start(offsets[:], offs)
             rows = keep.tile([P, T], U8, name=f"scale_rows{t}")
             nc.vector.memset(rows[:].bitcast(I32), 0)
             for o in range(PASSES):
@@ -48,11 +56,8 @@ def tile_picked_zhyb_sig_p_kernel(tc, x_words, x_scales, e_words, e_scales, hT, 
                 )
             scale_rows.append(rows)
 
-        raw = {}
-        for t, o in steps:
-            raw[t, o] = keep.tile([P, PACK * J], F32, name=f"raw{t}{o}")
-            rows = tables[t][2][o * K_PASS : (o + 1) * K_PASS, :]
-            nc.sync.dma_start(out=raw[t, o][:], in_=rows.rearrange("(p r) j -> p (r j)", r=PACK))
+        for t in range(TABLES):
+            load_queries(t, 1)
 
         words = {}
 
@@ -70,14 +75,12 @@ def tile_picked_zhyb_sig_p_kernel(tc, x_words, x_scales, e_words, e_scales, hT, 
         for t in range(TABLES):
             nc.vector.tensor_copy(picked_scales[:, t * S : (t + 1) * S], scale_rows[t][:].indirect(offsets[:]))
 
-        doc_scales = []
+        doc_scales = keep.tile([P, TABLES * S], U8, name="doc_scales", align_bytes=64)
+        nc.vector.tensor_copy(doc_scales[:].bitcast(I32), picked_scales[:].bitcast(I32))
         for o in range(PASSES):
-            planes = keep.tile([P, TABLES * S], U8, name=f"doc_scales{o}", align_bytes=64)
-            nc.vector.tensor_copy(planes[:].bitcast(I32), picked_scales[:].bitcast(I32))
-            doc_scales.append(planes)
             for i in range(1, ROWS):
                 nc.sync.dma_start(
-                    out=planes[ROWS * o + i : P : QUAD, :].bitcast(I32),
+                    out=doc_scales[ROWS * o + i : P : QUAD, :].bitcast(I32),
                     in_=picked_scales[ROWS * o + SPREAD * i : P : QUAD, :].bitcast(I32),
                 )
 
@@ -126,7 +129,7 @@ def tile_picked_zhyb_sig_p_kernel(tc, x_words, x_scales, e_words, e_scales, hT, 
                         lhsT=codes[t, o][:, m * P : (m + 1) * P].bitcast(FP8X4),
                         lhsT_scale=scales[t, o][:, m * P : (m + 1) * P],
                         rhs=doc_words[t, o][h].bitcast(FP8X4),
-                        rhs_scale=doc_scales[o][ROWS * o :, t * S + h * HALF : t * S + (h + 1) * HALF],
+                        rhs_scale=doc_scales[ROWS * o :, t * S + h * HALF : t * S + (h + 1) * HALF],
                         start=(t, o) == steps[0],
                         stop=(t, o) == steps[-1],
                     )

@@ -75,14 +75,17 @@ def tile_picked_zhyb_sig_p_kernel(tc, x_words, x_scales, e_words, e_scales, hT, 
         for t in range(TABLES):
             nc.vector.tensor_copy(picked_scales[:, t * S : (t + 1) * S], scale_rows[t][:].indirect(offsets[:]))
 
-        doc_scales = keep.tile([P, TABLES * S], U8, name="doc_scales", align_bytes=64)
-        nc.vector.tensor_copy(doc_scales[:].bitcast(I32), picked_scales[:].bitcast(I32))
-        for o in range(PASSES):
+        doc_scales = []
+
+        def place_scales(o, tag):
+            planes = keep.tile([P, TABLES * S], U8, name=f"doc_scales{o}", tag=tag, align_bytes=64)
+            nc.vector.tensor_copy(planes[:].bitcast(I32), picked_scales[:].bitcast(I32))
             for i in range(1, ROWS):
                 nc.sync.dma_start(
-                    out=doc_scales[ROWS * o + i : P : QUAD, :].bitcast(I32),
+                    out=planes[ROWS * o + i : P : QUAD, :].bitcast(I32),
                     in_=picked_scales[ROWS * o + SPREAD * i : P : QUAD, :].bitcast(I32),
                 )
+            doc_scales.append(planes)
 
         half_offsets = [offsets[:, h * (HALF // 16) : (h + 1) * (HALF // 16)] for h in range(2)]
         banks = {}
@@ -129,15 +132,17 @@ def tile_picked_zhyb_sig_p_kernel(tc, x_words, x_scales, e_words, e_scales, hT, 
                         lhsT=codes[t, o][:, m * P : (m + 1) * P].bitcast(FP8X4),
                         lhsT_scale=scales[t, o][:, m * P : (m + 1) * P],
                         rhs=doc_words[t, o][h].bitcast(FP8X4),
-                        rhs_scale=doc_scales[ROWS * o :, t * S + h * HALF : t * S + (h + 1) * HALF],
+                        rhs_scale=doc_scales[o][ROWS * o :, t * S + h * HALF : t * S + (h + 1) * HALF],
                         start=(t, o) == steps[0],
                         stop=(t, o) == steps[-1],
                     )
 
+        place_scales(0, "doc_scales0")
         for t, o in steps:
             quantise(t, o)
-        for t in range(TABLES):
-            load_words(t, 1, ["grouped10", "grouped01"][t])
+        load_words(0, 1, "grouped10")
+        place_scales(1, "grouped01")
+        load_words(1, 1, "grouped11")
         for t, o in steps:
             pick_words(t, o)
         for t, o in steps:

@@ -88,10 +88,8 @@ def tile_picked_zhyb_sig_p_kernel(tc, x_words, x_scales, e_words, e_scales, hT, 
             doc_scales.append(planes)
 
         half_offsets = [offsets[:, h * (HALF // 16) : (h + 1) * (HALF // 16)] for h in range(2)]
-        banks = {}
-        for h in range(2):
-            for m in range(J // P):
-                banks[h, m] = psum.tile([P, HALF], F32, name=f"bank{h}{m}")
+        pieces = [(0, 0, P), (0, P, P), (1, 0, HALF), (0, HALF, HALF), (1, HALF, HALF)]
+        banks = [psum.tile([P, width], F32, name=f"bank{n}") for n, (m, first, width) in enumerate(pieces)]
 
         doc_words = {}
         codes = {}
@@ -125,17 +123,17 @@ def tile_picked_zhyb_sig_p_kernel(tc, x_words, x_scales, e_words, e_scales, hT, 
             )
 
         def multiply(t, o):
-            for h in range(2):
-                for m in range(J // P):
-                    nc.tensor.matmul_mx(
-                        out=banks[h, m][:],
-                        lhsT=codes[t, o][:, m * P : (m + 1) * P].bitcast(FP8X4),
-                        lhsT_scale=scales[t, o][:, m * P : (m + 1) * P],
-                        rhs=doc_words[t, o][h].bitcast(FP8X4),
-                        rhs_scale=doc_scales[o][ROWS * o :, t * S + h * HALF : t * S + (h + 1) * HALF],
-                        start=(t, o) == steps[0],
-                        stop=(t, o) == steps[-1],
-                    )
+            for bank, (m, first, width) in zip(banks, pieces):
+                h, within = divmod(first, HALF)
+                nc.tensor.matmul_mx(
+                    out=bank[:],
+                    lhsT=codes[t, o][:, m * P : (m + 1) * P].bitcast(FP8X4),
+                    lhsT_scale=scales[t, o][:, m * P : (m + 1) * P],
+                    rhs=doc_words[t, o][h][:, within : within + width].bitcast(FP8X4),
+                    rhs_scale=doc_scales[o][ROWS * o :, t * S + first : t * S + first + width],
+                    start=(t, o) == steps[0],
+                    stop=(t, o) == steps[-1],
+                )
 
         place_scales(0, "doc_scales0")
         for t, o in steps:
@@ -148,8 +146,7 @@ def tile_picked_zhyb_sig_p_kernel(tc, x_words, x_scales, e_words, e_scales, hT, 
         for t, o in steps:
             multiply(t, o)
 
-        for h in range(2):
-            for m in range(J // P):
-                result = keep.tile([P, HALF], F32, name=f"result{h}{m}")
-                nc.scalar.activation(result[:], banks[h, m][:], SIGMOID)
-                nc.sync.dma_start(out=out[m * P : (m + 1) * P, h * HALF : (h + 1) * HALF], in_=result[:])
+        for n, (m, first, width) in enumerate(pieces):
+            result = keep.tile([P, width], F32, name=f"result{n}")
+            nc.scalar.activation(result[:], banks[n][:], SIGMOID)
+            nc.sync.dma_start(out=out[m * P : (m + 1) * P, first : first + width], in_=result[:])

@@ -34,6 +34,7 @@ def tile_picked_zhyb_sig_p_kernel(tc, x_words, x_scales, e_words, e_scales, hT, 
         offsets = keep.tile([P, S // 16], U16, name="offsets")
         tables = [(x_words, x_scales, hT), (e_words, e_scales, gT)]
         steps = [(t, o) for o in range(PASSES) for t in range(TABLES)]
+        products = [steps[1], steps[0]] + steps[2:]
 
         raw = {}
 
@@ -131,7 +132,7 @@ def tile_picked_zhyb_sig_p_kernel(tc, x_words, x_scales, e_words, e_scales, hT, 
                     lhsT_scale=scales[t, o][:, m * P : (m + 1) * P],
                     rhs=doc_words[t, o][h][:, within : within + width].bitcast(FP8X4),
                     rhs_scale=doc_scales[o][ROWS * o :, t * S + first : t * S + first + width],
-                    start=(t, o) == steps[0],
+                    start=(t, o) == products[0],
                     stop=(t, o) == steps[-1],
                 )
 
@@ -143,7 +144,7 @@ def tile_picked_zhyb_sig_p_kernel(tc, x_words, x_scales, e_words, e_scales, hT, 
         load_words(1, 1, "grouped11")
         for t, o in steps:
             pick_words(t, o)
-        for t, o in steps:
+        for t, o in products:
             multiply(t, o)
 
         for n, (m, first, width) in enumerate(pieces):

@@ -23,6 +23,7 @@ HALF = S // 2
 QUAD = 32
 ROWS = 4
 SPREAD = 8
+ALIGN = 512
 
 
 def tile_picked_zhyb_sig_p_kernel(tc, x_words, x_scales, e_words, e_scales, hT, gT, offs, out):
@@ -39,7 +40,7 @@ def tile_picked_zhyb_sig_p_kernel(tc, x_words, x_scales, e_words, e_scales, hT, 
         raw = {}
 
         def load_queries(t, o):
-            raw[t, o] = keep.tile([P, PACK * J], F32, name=f"raw{t}{o}")
+            raw[t, o] = keep.tile([P, PACK * J], F32, name=f"raw{t}{o}", align_bytes=ALIGN)
             rows = tables[t][2][o * K_PASS : (o + 1) * K_PASS, :]
             nc.sync.dma_start(out=raw[t, o][:], in_=rows.rearrange("(p r) j -> p (r j)", r=PACK))
 
@@ -48,7 +49,7 @@ def tile_picked_zhyb_sig_p_kernel(tc, x_words, x_scales, e_words, e_scales, hT, 
             load_queries(t, 0)
             if t == 0:
                 nc.sync.dma_start(offsets[:], offs)
-            rows = keep.tile([P, T], U8, name=f"scale_rows{t}")
+            rows = keep.tile([P, T], U8, name=f"scale_rows{t}", align_bytes=ALIGN)
             nc.vector.memset(rows[:].bitcast(I32), 0)
             for o in range(PASSES):
                 nc.sync.dma_start(
@@ -63,7 +64,7 @@ def tile_picked_zhyb_sig_p_kernel(tc, x_words, x_scales, e_words, e_scales, hT, 
         words = {}
 
         def load_words(t, o, tag):
-            words[t, o] = keep.tile([P, T], U32, name=f"words{t}{o}", tag=tag, align_bytes=64)
+            words[t, o] = keep.tile([P, T], U32, name=f"words{t}{o}", tag=tag, align_bytes=ALIGN)
             nc.sync.dma_start(
                 out=words[t, o][:].bitcast(I32),
                 in_=tables[t][0][o].rearrange("p n r -> p (n r)").bitcast(I32),
@@ -72,14 +73,14 @@ def tile_picked_zhyb_sig_p_kernel(tc, x_words, x_scales, e_words, e_scales, hT, 
         for t in range(TABLES):
             load_words(t, 0, f"words{t}0")
 
-        picked_scales = keep.tile([P, TABLES * S], U8, name="picked_scales", align_bytes=64)
+        picked_scales = keep.tile([P, TABLES * S], U8, name="picked_scales", align_bytes=ALIGN)
         for t in range(TABLES):
             nc.vector.tensor_copy(picked_scales[:, t * S : (t + 1) * S], scale_rows[t][:].indirect(offsets[:]))
 
         doc_scales = []
 
         def place_scales(o, tag):
-            planes = keep.tile([P, TABLES * S], U8, name=f"doc_scales{o}", tag=tag, align_bytes=64)
+            planes = keep.tile([P, TABLES * S], U8, name=f"doc_scales{o}", tag=tag, align_bytes=ALIGN)
             nc.vector.tensor_copy(planes[:].bitcast(I32), picked_scales[:].bitcast(I32))
             for i in range(1, ROWS):
                 nc.sync.dma_start(
@@ -100,23 +101,23 @@ def tile_picked_zhyb_sig_p_kernel(tc, x_words, x_scales, e_words, e_scales, hT, 
             if (t, o) == steps[-1]:
                 halves = []
                 for h in range(2):
-                    picked = keep.tile([P, HALF], U32, name=f"picked_last{h}", align_bytes=64)
+                    picked = keep.tile([P, HALF], U32, name=f"picked_last{h}", align_bytes=ALIGN)
                     nc.vector.tensor_copy(picked[:], words[t, o][:].indirect(half_offsets[h]))
                     halves.append(picked[:])
             else:
-                picked = keep.tile([P, S], U32, name=f"picked{t}{o}", align_bytes=64)
+                picked = keep.tile([P, S], U32, name=f"picked{t}{o}", align_bytes=ALIGN)
                 nc.vector.tensor_copy(picked[:], words[t, o][:].indirect(offsets[:]))
                 halves = [picked[:, h * HALF : (h + 1) * HALF] for h in range(2)]
             doc_words[t, o] = halves
 
         def quantise(t, o):
-            grouped = keep.tile([P, J, PACK], BF16, name=f"grouped{t}{o}", tag=f"grouped{t}{o}", align_bytes=64)
+            grouped = keep.tile([P, J, PACK], BF16, name=f"grouped{t}{o}", tag=f"grouped{t}{o}", align_bytes=ALIGN)
             nc.scalar.copy(
                 out=grouped[:].rearrange("p (c i) r -> p c r i", i=4),
                 in_=raw[t, o][:].rearrange("p (r c i) -> p c r i", r=PACK, i=4),
             )
-            codes[t, o] = keep.tile([P, J], U32, name=f"codes{t}{o}", align_bytes=64)
-            scales[t, o] = keep.tile([P, J], U8, name=f"scales{t}{o}", align_bytes=64)
+            codes[t, o] = keep.tile([P, J], U32, name=f"codes{t}{o}", align_bytes=ALIGN)
+            scales[t, o] = keep.tile([P, J], U8, name=f"scales{t}{o}", align_bytes=ALIGN)
             nc.vector.quantize_mx(
                 out=codes[t, o][:].bitcast(FP8X4),
                 scales=scales[t, o][:],
@@ -148,6 +149,6 @@ def tile_picked_zhyb_sig_p_kernel(tc, x_words, x_scales, e_words, e_scales, hT, 
             multiply(t, o)
 
         for n, (m, first, width) in enumerate(pieces):
-            result = keep.tile([P, width], F32, name=f"result{n}")
+            result = keep.tile([P, width], F32, name=f"result{n}", align_bytes=ALIGN)
             nc.scalar.activation(result[:], banks[n][:], SIGMOID)
             nc.sync.dma_start(out=out[m * P : (m + 1) * P, first : first + width], in_=result[:])

@@ -124,9 +124,11 @@ def tile_picked_zhyb_sig_p_kernel(tc, x_words, x_scales, e_words, e_scales, hT, 
                 in_=grouped[:].rearrange("p j r -> p (j r)"),
             )
 
-        def multiply(t, o):
+        def multiply(t, o, halves):
             for bank, (m, first, width) in zip(banks, pieces):
                 h, within = divmod(first, HALF)
+                if h not in halves:
+                    continue
                 nc.tensor.matmul_mx(
                     out=bank[:],
                     lhsT=codes[t, o][:, m * P : (m + 1) * P].bitcast(FP8X4),
@@ -141,12 +143,17 @@ def tile_picked_zhyb_sig_p_kernel(tc, x_words, x_scales, e_words, e_scales, hT, 
         for t, o in steps:
             quantise(t, o)
         load_words(0, 1, "grouped10")
-        place_scales(1, "grouped01")
         load_words(1, 1, "grouped11")
-        for t, o in steps:
+        for t, o in steps[:2]:
             pick_words(t, o)
-        for t, o in products:
-            multiply(t, o)
+        place_scales(1, "words00")
+        for t, o in steps[2:]:
+            pick_words(t, o)
+        for t, o in products[:2]:
+            multiply(t, o, (0, 1))
+        for h in range(2):
+            for t, o in products[2:]:
+                multiply(t, o, (h,))
 
         for n, (m, first, width) in enumerate(pieces):
             result = keep.tile([P, width], F32, name=f"result{n}", align_bytes=ALIGN)

@@ -35,7 +35,7 @@ def tile_picked_zhyb_sig_p_kernel(tc, x_words, x_scales, e_words, e_scales, hT, 
         offsets = keep.tile([P, S // 16], U16, name="offsets")
         tables = [(x_words, x_scales, hT), (e_words, e_scales, gT)]
         steps = [(t, o) for o in range(PASSES) for t in range(TABLES)]
-        products = [steps[1], steps[0]] + steps[2:]
+        word_order = [(0, 1), (0, 0), (1, 0), (1, 1)]
 
         raw = {}
 
@@ -70,8 +70,8 @@ def tile_picked_zhyb_sig_p_kernel(tc, x_words, x_scales, e_words, e_scales, hT, 
                 in_=tables[t][0][o].rearrange("p n r -> p (n r)").bitcast(I32),
             )
 
-        for t in range(TABLES):
-            load_words(t, 0, f"words{t}0")
+        for t, o in word_order[:2]:
+            load_words(t, o, f"words{t}{o}")
 
         picked_scales = keep.tile([P, TABLES * S], U8, name="picked_scales", align_bytes=ALIGN)
         for t in range(TABLES):
@@ -98,10 +98,10 @@ def tile_picked_zhyb_sig_p_kernel(tc, x_words, x_scales, e_words, e_scales, hT, 
         scales = {}
 
         def pick_words(t, o):
-            if (t, o) == steps[-1]:
+            if t == 1:
                 halves = []
                 for h in range(2):
-                    picked = keep.tile([P, HALF], U32, name=f"picked_last{h}", align_bytes=ALIGN)
+                    picked = keep.tile([P, HALF], U32, name=f"picked{t}{o}{h}", align_bytes=ALIGN)
                     nc.vector.tensor_copy(picked[:], words[t, o][:].indirect(half_offsets[h]))
                     halves.append(picked[:])
             else:
@@ -135,24 +135,23 @@ def tile_picked_zhyb_sig_p_kernel(tc, x_words, x_scales, e_words, e_scales, hT, 
                     lhsT_scale=scales[t, o][:, m * P : (m + 1) * P],
                     rhs=doc_words[t, o][h][:, within : within + width].bitcast(FP8X4),
                     rhs_scale=doc_scales[o][ROWS * o :, t * S + first : t * S + first + width],
-                    start=(t, o) == products[0],
+                    start=(t, o) == steps[0],
                     stop=(t, o) == steps[-1],
                 )
 
         place_scales(0, "doc_scales0")
         for t, o in steps:
             quantise(t, o)
-        load_words(0, 1, "grouped10")
+        load_words(1, 0, "grouped10")
         load_words(1, 1, "grouped11")
+        pick_words(0, 1)
+        place_scales(1, "words01")
+        for t, o in word_order[1:]:
+            pick_words(t, o)
         for t, o in steps[:2]:
-            pick_words(t, o)
-        place_scales(1, "words00")
-        for t, o in steps[2:]:
-            pick_words(t, o)
-        for t, o in products[:2]:
             multiply(t, o, (0, 1))
         for h in range(2):
-            for t, o in products[2:]:
+            for t, o in steps[2:]:
                 multiply(t, o, (h,))
 
         for n, (m, first, width) in enumerate(pieces):

@@ -18,12 +18,12 @@ P = 128
 PACK = 4
 K_PASS = P * PACK
 PASSES = K // K_PASS
-TABLES = 2
 HALF = S // 2
 QUAD = 32
 ROWS = 4
 SPREAD = 8
 ALIGN = 512
+X, E = 0, 1
 
 
 def tile_picked_zhyb_sig_p_kernel(tc, x_words, x_scales, e_words, e_scales, hT, gT, offs, out):
@@ -32,129 +32,139 @@ def tile_picked_zhyb_sig_p_kernel(tc, x_words, x_scales, e_words, e_scales, hT, 
         keep = ctx.enter_context(tc.tile_pool(name="keep", bufs=1))
         psum = ctx.enter_context(tc.psum_pool(name="psum", bufs=1))
 
-        offsets = keep.tile([P, S // 16], U16, name="offsets")
-        tables = [(x_words, x_scales, hT), (e_words, e_scales, gT)]
-        steps = [(t, o) for o in range(PASSES) for t in range(TABLES)]
-        word_order = [(0, 1), (0, 0), (1, 0), (1, 1)]
+        def tile(shape, dtype, name, tag=None):
+            return keep.tile(shape, dtype, name=name, tag=tag or name, align_bytes=ALIGN)
+
+        words_in = {X: x_words, E: e_words}
+        scales_in = {X: x_scales, E: e_scales}
+        queries_in = {X: hT, E: gT}
 
         raw = {}
 
-        def load_queries(t, o):
-            raw[t, o] = keep.tile([P, PACK * J], F32, name=f"raw{t}{o}", align_bytes=ALIGN)
-            rows = tables[t][2][o * K_PASS : (o + 1) * K_PASS, :]
-            nc.sync.dma_start(out=raw[t, o][:], in_=rows.rearrange("(p r) j -> p (r j)", r=PACK))
-
-        scale_rows = []
-        for t in range(TABLES):
-            load_queries(t, 0)
-            if t == 0:
-                nc.sync.dma_start(offsets[:], offs)
-            rows = keep.tile([P, T], U8, name=f"scale_rows{t}", align_bytes=ALIGN)
-            nc.vector.memset(rows[:].bitcast(I32), 0)
+        def load_queries(t):
+            both = tile([P, PASSES, PACK * J], F32, f"raw{t}")
+            nc.sync.dma_start(out=both[:], in_=queries_in[t].rearrange("(o p r) j -> p o (r j)", o=PASSES, r=PACK))
             for o in range(PASSES):
-                nc.sync.dma_start(
-                    out=rows[ROWS * o : P : SPREAD, :].bitcast(I32),
-                    in_=tables[t][1][o].bitcast(I32),
-                )
-            scale_rows.append(rows)
+                raw[t, o] = both[:, o, :]
 
-        for t in range(TABLES):
-            load_queries(t, 1)
+        def load_query_pass(t, o):
+            one = tile([P, PACK * J], F32, f"raw{t}{o}")
+            nc.sync.dma_start(out=one[:], in_=queries_in[t].rearrange("(o p r) j -> o p (r j)", o=PASSES, r=PACK)[o])
+            raw[t, o] = one[:]
+
+        scale_rows = {}
+
+        def load_scale_rows(t):
+            scale_rows[t] = tile([P, T], U8, f"scale_rows{t}")
+            nc.vector.memset(scale_rows[t][:].bitcast(I32), 0)
+            nc.sync.dma_start(
+                out=scale_rows[t][0:P:ROWS, :].bitcast(I32),
+                in_=scales_in[t].bitcast(I32).rearrange("o q n -> q o n"),
+            )
 
         words = {}
 
-        def load_words(t, o, tag):
-            words[t, o] = keep.tile([P, T], U32, name=f"words{t}{o}", tag=tag, align_bytes=ALIGN)
+        def load_words(t, o, tag=None):
+            words[t, o] = tile([P, T], U32, f"words{t}{o}", tag)
             nc.sync.dma_start(
                 out=words[t, o][:].bitcast(I32),
-                in_=tables[t][0][o].rearrange("p n r -> p (n r)").bitcast(I32),
+                in_=words_in[t][o].rearrange("p n r -> p (n r)").bitcast(I32),
             )
 
-        for t, o in word_order[:2]:
-            load_words(t, o, f"words{t}{o}")
+        load_query_pass(X, 0)
+        offsets = keep.tile([P, S // 16], U16, name="offsets")
+        nc.sync.dma_start(offsets[:], offs)
+        load_scale_rows(X)
+        load_query_pass(X, 1)
+        load_scale_rows(E)
+        load_queries(E)
+        load_words(X, 1)
+        load_words(X, 0)
 
-        picked_scales = keep.tile([P, TABLES * S], U8, name="picked_scales", align_bytes=ALIGN)
-        for t in range(TABLES):
+        picked_scales = tile([P, 2 * S], U8, "picked_scales")
+        for t in (X, E):
             nc.vector.tensor_copy(picked_scales[:, t * S : (t + 1) * S], scale_rows[t][:].indirect(offsets[:]))
 
-        doc_scales = []
+        planes = {}
 
-        def place_scales(o, tag):
-            planes = keep.tile([P, TABLES * S], U8, name=f"doc_scales{o}", tag=tag, align_bytes=ALIGN)
-            nc.vector.tensor_copy(planes[:].bitcast(I32), picked_scales[:].bitcast(I32))
-            for i in range(1, ROWS):
-                nc.sync.dma_start(
-                    out=planes[ROWS * o + i : P : QUAD, :].bitcast(I32),
-                    in_=picked_scales[ROWS * o + SPREAD * i : P : QUAD, :].bitcast(I32),
-                )
-            doc_scales.append(planes)
+        def place_scales(o, spans, tag=None):
+            planes[o] = tile([P, 2 * S], U8, f"planes{o}", tag)
+            nc.vector.tensor_copy(planes[o][:].bitcast(I32), picked_scales[:].bitcast(I32))
+            for span in spans:
+                for i in range(1, ROWS):
+                    nc.sync.dma_start(
+                        out=planes[o][ROWS * o + i : P : QUAD, span].bitcast(I32),
+                        in_=picked_scales[ROWS * o + SPREAD * i : P : QUAD, span].bitcast(I32),
+                    )
 
-        half_offsets = [offsets[:, h * (HALF // 16) : (h + 1) * (HALF // 16)] for h in range(2)]
-        pieces = [(0, 0, P), (0, P, P), (1, 0, HALF), (0, HALF, HALF), (1, HALF, HALF)]
-        banks = [psum.tile([P, width], F32, name=f"bank{n}") for n, (m, first, width) in enumerate(pieces)]
-
-        doc_words = {}
         codes = {}
         scales = {}
 
-        def pick_words(t, o):
-            if t == 1:
-                halves = []
-                for h in range(2):
-                    picked = keep.tile([P, HALF], U32, name=f"picked{t}{o}{h}", align_bytes=ALIGN)
-                    nc.vector.tensor_copy(picked[:], words[t, o][:].indirect(half_offsets[h]))
-                    halves.append(picked[:])
-            else:
-                picked = keep.tile([P, S], U32, name=f"picked{t}{o}", align_bytes=ALIGN)
-                nc.vector.tensor_copy(picked[:], words[t, o][:].indirect(offsets[:]))
-                halves = [picked[:, h * HALF : (h + 1) * HALF] for h in range(2)]
-            doc_words[t, o] = halves
-
         def quantise(t, o):
-            grouped = keep.tile([P, J, PACK], BF16, name=f"grouped{t}{o}", tag=f"grouped{t}{o}", align_bytes=ALIGN)
+            grouped = tile([P, J, PACK], BF16, f"grouped{t}{o}")
             nc.scalar.copy(
                 out=grouped[:].rearrange("p (c i) r -> p c r i", i=4),
-                in_=raw[t, o][:].rearrange("p (r c i) -> p c r i", r=PACK, i=4),
+                in_=raw[t, o].rearrange("p (r c i) -> p c r i", r=PACK, i=4),
             )
-            codes[t, o] = keep.tile([P, J], U32, name=f"codes{t}{o}", align_bytes=ALIGN)
-            scales[t, o] = keep.tile([P, J], U8, name=f"scales{t}{o}", align_bytes=ALIGN)
+            codes[t, o] = tile([P, J], U32, f"codes{t}{o}")
+            scales[t, o] = tile([P, J], U8, f"scales{t}{o}")
             nc.vector.quantize_mx(
                 out=codes[t, o][:].bitcast(FP8X4),
                 scales=scales[t, o][:],
                 in_=grouped[:].rearrange("p j r -> p (j r)"),
             )
 
-        def multiply(t, o, halves):
-            for bank, (m, first, width) in zip(banks, pieces):
-                h, within = divmod(first, HALF)
-                if h not in halves:
-                    continue
-                nc.tensor.matmul_mx(
-                    out=bank[:],
-                    lhsT=codes[t, o][:, m * P : (m + 1) * P].bitcast(FP8X4),
-                    lhsT_scale=scales[t, o][:, m * P : (m + 1) * P],
-                    rhs=doc_words[t, o][h][:, within : within + width].bitcast(FP8X4),
-                    rhs_scale=doc_scales[o][ROWS * o :, t * S + first : t * S + first + width],
-                    start=(t, o) == steps[0],
-                    stop=(t, o) == steps[-1],
-                )
+        picked = {}
 
-        place_scales(0, "doc_scales0")
-        for t, o in steps:
-            quantise(t, o)
-        load_words(1, 0, "grouped10")
-        load_words(1, 1, "grouped11")
-        pick_words(0, 1)
-        place_scales(1, "words01")
-        for t, o in word_order[1:]:
-            pick_words(t, o)
-        for t, o in steps[:2]:
-            multiply(t, o, (0, 1))
+        def pick_whole(t, o):
+            whole = tile([P, S], U32, f"picked{t}{o}")
+            nc.vector.tensor_copy(whole[:], words[t, o][:].indirect(offsets[:]))
+            for h in range(2):
+                picked[t, o, h] = whole[:, h * HALF : (h + 1) * HALF]
+
+        def pick_halves(t, o):
+            for h in range(2):
+                half = tile([P, HALF], U32, f"picked{t}{o}{h}")
+                nc.vector.tensor_copy(half[:], words[t, o][:].indirect(offsets[:, h * (HALF // 16) : (h + 1) * (HALF // 16)]))
+                picked[t, o, h] = half[:]
+
+        pieces = [(0, 0, P), (0, P, P), (1, 0, HALF), (0, HALF, HALF), (1, HALF, HALF)]
+        banks = [psum.tile([P, width], F32, name=f"bank{n}") for n, (m, first, width) in enumerate(pieces)]
+
+        def multiply(t, o, h):
+            for bank, (m, first, width) in zip(banks, pieces):
+                if first // HALF == h:
+                    within = first % HALF
+                    nc.tensor.matmul_mx(
+                        out=bank[:],
+                        lhsT=codes[t, o][:, m * P : (m + 1) * P].bitcast(FP8X4),
+                        lhsT_scale=scales[t, o][:, m * P : (m + 1) * P],
+                        rhs=picked[t, o, h][:, within : within + width].bitcast(FP8X4),
+                        rhs_scale=planes[o][ROWS * o :, t * S + first : t * S + first + width],
+                        start=(t, o) == (X, 0),
+                        stop=(t, o) == (E, 1),
+                    )
+
+        place_scales(0, [slice(0, 2 * S)])
+        quantise(X, 0)
+        quantise(X, 1)
+        load_words(E, 0, "grouped00")
+        load_words(E, 1, "grouped01")
+        quantise(E, 0)
+        quantise(E, 1)
+        pick_whole(X, 1)
+        place_scales(1, [slice(0, S), slice(S, 2 * S)], "words01")
+        pick_whole(X, 0)
+        pick_halves(E, 0)
+        pick_halves(E, 1)
+        for t in (X, E):
+            for h in range(2):
+                multiply(t, 0, h)
         for h in range(2):
-            for t, o in steps[2:]:
-                multiply(t, o, (h,))
+            for t in (X, E):
+                multiply(t, 1, h)
 
         for n, (m, first, width) in enumerate(pieces):
-            result = keep.tile([P, width], F32, name=f"result{n}", align_bytes=ALIGN)
+            result = tile([P, width], F32, f"result{n}")
             nc.scalar.activation(result[:], banks[n][:], SIGMOID)
             nc.sync.dma_start(out=out[m * P : (m + 1) * P, first : first + width], in_=result[:])

@@ -35,17 +35,17 @@ def tile_picked_zhyb_sig_p_kernel(tc, x_words, x_scales, e_words, e_scales, hT, 
         def tile(shape, dtype, name, tag=None):
             return keep.tile(shape, dtype, name=name, tag=tag or name, align_bytes=ALIGN)
 
+        offsets = keep.tile([P, S // 16], U16, name="offsets")
+
+        def shifted(width, dtype, per_line, lines, name):
+            whole = tile([P, per_line * lines + width], dtype, name)
+            return whole[:, per_line * lines :]
+
         words_in = {X: x_words, E: e_words}
         scales_in = {X: x_scales, E: e_scales}
         queries_in = {X: hT, E: gT}
 
         raw = {}
-
-        def load_queries(t):
-            both = tile([P, PASSES, PACK * J], F32, f"raw{t}")
-            nc.sync.dma_start(out=both[:], in_=queries_in[t].rearrange("(o p r) j -> p o (r j)", o=PASSES, r=PACK))
-            for o in range(PASSES):
-                raw[t, o] = both[:, o, :]
 
         def load_query_pass(t, o):
             one = tile([P, PACK * J], F32, f"raw{t}{o}")
@@ -57,10 +57,11 @@ def tile_picked_zhyb_sig_p_kernel(tc, x_words, x_scales, e_words, e_scales, hT, 
         def load_scale_rows(t):
             scale_rows[t] = tile([P, T], U8, f"scale_rows{t}")
             nc.vector.memset(scale_rows[t][:].bitcast(I32), 0)
-            nc.sync.dma_start(
-                out=scale_rows[t][0:P:ROWS, :].bitcast(I32),
-                in_=scales_in[t].bitcast(I32).rearrange("o q n -> q o n"),
-            )
+            for o in range(PASSES):
+                nc.sync.dma_start(
+                    out=scale_rows[t][ROWS * o : P : SPREAD, :].bitcast(I32),
+                    in_=scales_in[t][o].bitcast(I32),
+                )
 
         words = {}
 
@@ -72,12 +73,12 @@ def tile_picked_zhyb_sig_p_kernel(tc, x_words, x_scales, e_words, e_scales, hT, 
             )
 
         load_query_pass(X, 0)
-        offsets = keep.tile([P, S // 16], U16, name="offsets")
         nc.sync.dma_start(offsets[:], offs)
         load_scale_rows(X)
-        load_query_pass(X, 1)
+        load_query_pass(E, 0)
         load_scale_rows(E)
-        load_queries(E)
+        load_query_pass(X, 1)
+        load_query_pass(E, 1)
         load_words(X, 1)
         load_words(X, 0)
 
@@ -87,15 +88,14 @@ def tile_picked_zhyb_sig_p_kernel(tc, x_words, x_scales, e_words, e_scales, hT, 
 
         planes = {}
 
-        def place_scales(o, spans, tag=None):
+        def place_scales(o, tag=None):
             planes[o] = tile([P, 2 * S], U8, f"planes{o}", tag)
             nc.vector.tensor_copy(planes[o][:].bitcast(I32), picked_scales[:].bitcast(I32))
-            for span in spans:
-                for i in range(1, ROWS):
-                    nc.sync.dma_start(
-                        out=planes[o][ROWS * o + i : P : QUAD, span].bitcast(I32),
-                        in_=picked_scales[ROWS * o + SPREAD * i : P : QUAD, span].bitcast(I32),
-                    )
+            for i in range(1, ROWS):
+                nc.sync.dma_start(
+                    out=planes[o][ROWS * o + i : P : QUAD, :].bitcast(I32),
+                    in_=picked_scales[ROWS * o + SPREAD * i : P : QUAD, :].bitcast(I32),
+                )
 
         codes = {}
         scales = {}
@@ -106,27 +106,27 @@ def tile_picked_zhyb_sig_p_kernel(tc, x_words, x_scales, e_words, e_scales, hT, 
                 out=grouped[:].rearrange("p (c i) r -> p c r i", i=4),
                 in_=raw[t, o].rearrange("p (r c i) -> p c r i", r=PACK, i=4),
             )
-            codes[t, o] = tile([P, J], U32, f"codes{t}{o}")
-            scales[t, o] = tile([P, J], U8, f"scales{t}{o}")
+            codes[t, o] = shifted(J, U32, 16, 2, f"codes{t}{o}")
+            scales[t, o] = shifted(J, U8, 64, 3, f"scales{t}{o}")
             nc.vector.quantize_mx(
-                out=codes[t, o][:].bitcast(FP8X4),
-                scales=scales[t, o][:],
+                out=codes[t, o].bitcast(FP8X4),
+                scales=scales[t, o],
                 in_=grouped[:].rearrange("p j r -> p (j r)"),
             )
 
         picked = {}
 
         def pick_whole(t, o):
-            whole = tile([P, S], U32, f"picked{t}{o}")
-            nc.vector.tensor_copy(whole[:], words[t, o][:].indirect(offsets[:]))
+            whole = shifted(S, U32, 16, 1, f"picked{t}{o}")
+            nc.vector.tensor_copy(whole, words[t, o][:].indirect(offsets[:]))
             for h in range(2):
                 picked[t, o, h] = whole[:, h * HALF : (h + 1) * HALF]
 
         def pick_halves(t, o):
             for h in range(2):
-                half = tile([P, HALF], U32, f"picked{t}{o}{h}")
-                nc.vector.tensor_copy(half[:], words[t, o][:].indirect(offsets[:, h * (HALF // 16) : (h + 1) * (HALF // 16)]))
-                picked[t, o, h] = half[:]
+                half = shifted(HALF, U32, 16, 1, f"picked{t}{o}{h}")
+                nc.vector.tensor_copy(half, words[t, o][:].indirect(offsets[:, h * (HALF // 16) : (h + 1) * (HALF // 16)]))
+                picked[t, o, h] = half
 
         pieces = [(0, 0, P), (0, P, P), (1, 0, HALF), (0, HALF, HALF), (1, HALF, HALF)]
         banks = [psum.tile([P, width], F32, name=f"bank{n}") for n, (m, first, width) in enumerate(pieces)]
@@ -145,15 +145,15 @@ def tile_picked_zhyb_sig_p_kernel(tc, x_words, x_scales, e_words, e_scales, hT, 
                         stop=(t, o) == (E, 1),
                     )
 
-        place_scales(0, [slice(0, 2 * S)])
+        place_scales(0)
         quantise(X, 0)
-        quantise(X, 1)
-        load_words(E, 0, "grouped00")
-        load_words(E, 1, "grouped01")
         quantise(E, 0)
+        quantise(X, 1)
         quantise(E, 1)
+        load_words(E, 0, "grouped10")
+        load_words(E, 1, "grouped11")
         pick_whole(X, 1)
-        place_scales(1, [slice(0, S), slice(S, 2 * S)], "words01")
+        place_scales(1, "words01")
         pick_whole(X, 0)
         pick_halves(E, 0)
         pick_halves(E, 1)

@@ -18,7 +18,9 @@ P = 128
 PACK = 4
 K_PASS = P * PACK
 PASSES = K // K_PASS
-HALF = S // 2
+QUARTERS = 4
+QUARTER = S // QUARTERS
+STRIPE = 16
 QUAD = 32
 ROWS = 4
 SPREAD = 8
@@ -35,11 +37,7 @@ def tile_picked_zhyb_sig_p_kernel(tc, x_words, x_scales, e_words, e_scales, hT, 
         def tile(shape, dtype, name, tag=None):
             return keep.tile(shape, dtype, name=name, tag=tag or name, align_bytes=ALIGN)
 
-        offsets = keep.tile([P, S // 16], U16, name="offsets")
-
-        def shifted(width, dtype, per_line, lines, name):
-            whole = tile([P, per_line * lines + width], dtype, name)
-            return whole[:, per_line * lines :]
+        offsets = keep.tile([P, S // STRIPE], U16, name="offsets")
 
         words_in = {X: x_words, E: e_words}
         scales_in = {X: x_scales, E: e_scales}
@@ -47,10 +45,9 @@ def tile_picked_zhyb_sig_p_kernel(tc, x_words, x_scales, e_words, e_scales, hT, 
 
         raw = {}
 
-        def load_query_pass(t, o):
-            one = tile([P, PACK * J], F32, f"raw{t}{o}")
-            nc.sync.dma_start(out=one[:], in_=queries_in[t].rearrange("(o p r) j -> o p (r j)", o=PASSES, r=PACK)[o])
-            raw[t, o] = one[:]
+        def load_queries(t, o):
+            raw[t, o] = tile([P, PACK * J], F32, f"raw{t}{o}")
+            nc.sync.dma_start(out=raw[t, o][:], in_=queries_in[t].rearrange("(o p r) j -> o p (r j)", o=PASSES, r=PACK)[o])
 
         scale_rows = {}
 
@@ -72,28 +69,26 @@ def tile_picked_zhyb_sig_p_kernel(tc, x_words, x_scales, e_words, e_scales, hT, 
                 in_=words_in[t][o].rearrange("p n r -> p (n r)").bitcast(I32),
             )
 
-        load_query_pass(X, 0)
+        load_queries(X, 0)
         nc.sync.dma_start(offsets[:], offs)
         load_scale_rows(X)
-        load_query_pass(E, 0)
+        load_queries(E, 0)
         load_scale_rows(E)
-        load_query_pass(X, 1)
-        load_query_pass(E, 1)
-        load_words(X, 1)
+        load_queries(X, 1)
+        load_queries(E, 1)
         load_words(X, 0)
+        load_words(X, 1)
 
         picked_scales = tile([P, 2 * S], U8, "picked_scales")
         for t in (X, E):
             nc.vector.tensor_copy(picked_scales[:, t * S : (t + 1) * S], scale_rows[t][:].indirect(offsets[:]))
 
-        planes = {}
-
-        def place_scales(o, tag=None):
-            planes[o] = tile([P, 2 * S], U8, f"planes{o}", tag)
-            nc.vector.tensor_copy(planes[o][:].bitcast(I32), picked_scales[:].bitcast(I32))
+        planes = tile([P, 2 * S], U8, "planes")
+        nc.vector.tensor_copy(planes[:].bitcast(I32), picked_scales[:].bitcast(I32))
+        for o in range(PASSES):
             for i in range(1, ROWS):
                 nc.sync.dma_start(
-                    out=planes[o][ROWS * o + i : P : QUAD, :].bitcast(I32),
+                    out=planes[ROWS * o + i : P : QUAD, :].bitcast(I32),
                     in_=picked_scales[ROWS * o + SPREAD * i : P : QUAD, :].bitcast(I32),
                 )
 
@@ -104,67 +99,65 @@ def tile_picked_zhyb_sig_p_kernel(tc, x_words, x_scales, e_words, e_scales, hT, 
             grouped = tile([P, J, PACK], BF16, f"grouped{t}{o}")
             nc.scalar.copy(
                 out=grouped[:].rearrange("p (c i) r -> p c r i", i=4),
-                in_=raw[t, o].rearrange("p (r c i) -> p c r i", r=PACK, i=4),
+                in_=raw[t, o][:].rearrange("p (r c i) -> p c r i", r=PACK, i=4),
             )
-            codes[t, o] = shifted(J, U32, 16, 2, f"codes{t}{o}")
-            scales[t, o] = shifted(J, U8, 64, 3, f"scales{t}{o}")
+            codes[t, o] = tile([P, J], U32, f"codes{t}{o}")
+            scales[t, o] = tile([P, J], U8, f"scales{t}{o}")
             nc.vector.quantize_mx(
-                out=codes[t, o].bitcast(FP8X4),
-                scales=scales[t, o],
+                out=codes[t, o][:].bitcast(FP8X4),
+                scales=scales[t, o][:],
                 in_=grouped[:].rearrange("p j r -> p (j r)"),
             )
 
-        picked = {}
-
-        def pick_whole(t, o):
-            whole = shifted(S, U32, 16, 1, f"picked{t}{o}")
-            nc.vector.tensor_copy(whole, words[t, o][:].indirect(offsets[:]))
-            for h in range(2):
-                picked[t, o, h] = whole[:, h * HALF : (h + 1) * HALF]
-
-        def pick_halves(t, o):
-            for h in range(2):
-                half = shifted(HALF, U32, 16, 1, f"picked{t}{o}{h}")
-                nc.vector.tensor_copy(half, words[t, o][:].indirect(offsets[:, h * (HALF // 16) : (h + 1) * (HALF // 16)]))
-                picked[t, o, h] = half
-
-        pieces = [(0, 0, P), (0, P, P), (1, 0, HALF), (0, HALF, HALF), (1, HALF, HALF)]
-        banks = [psum.tile([P, width], F32, name=f"bank{n}") for n, (m, first, width) in enumerate(pieces)]
-
-        def multiply(t, o, h):
-            for bank, (m, first, width) in zip(banks, pieces):
-                if first // HALF == h:
-                    within = first % HALF
-                    nc.tensor.matmul_mx(
-                        out=bank[:],
-                        lhsT=codes[t, o][:, m * P : (m + 1) * P].bitcast(FP8X4),
-                        lhsT_scale=scales[t, o][:, m * P : (m + 1) * P],
-                        rhs=picked[t, o, h][:, within : within + width].bitcast(FP8X4),
-                        rhs_scale=planes[o][ROWS * o :, t * S + first : t * S + first + width],
-                        start=(t, o) == (X, 0),
-                        stop=(t, o) == (E, 1),
-                    )
-
-        place_scales(0)
-        quantise(X, 0)
-        quantise(E, 0)
-        quantise(X, 1)
-        quantise(E, 1)
+        for o in range(PASSES):
+            for t in (X, E):
+                quantise(t, o)
         load_words(E, 0, "grouped10")
         load_words(E, 1, "grouped11")
-        pick_whole(X, 1)
-        place_scales(1, "words01")
-        pick_whole(X, 0)
-        pick_halves(E, 0)
-        pick_halves(E, 1)
-        for t in (X, E):
-            for h in range(2):
-                multiply(t, 0, h)
-        for h in range(2):
-            for t in (X, E):
-                multiply(t, 1, h)
 
-        for n, (m, first, width) in enumerate(pieces):
-            result = tile([P, width], F32, f"result{n}")
-            nc.scalar.activation(result[:], banks[n][:], SIGMOID)
-            nc.sync.dma_start(out=out[m * P : (m + 1) * P, first : first + width], in_=result[:])
+        picked = {}
+
+        def pick(t, o, parts):
+            width = S // parts
+            for part in range(parts):
+                one = tile([P, width], U32, f"picked{t}{o}{part}")
+                columns = slice(part * width // STRIPE, (part + 1) * width // STRIPE)
+                nc.vector.tensor_copy(one[:], words[t, o][:].indirect(offsets[:, columns]))
+                for n in range(width // QUARTER):
+                    picked[t, o, part * width // QUARTER + n] = one[:, n * QUARTER : (n + 1) * QUARTER]
+
+        order = [(0, 0), (1, 0), (1, 1), (0, 1), (0, 2), (1, 2), (1, 3), (0, 3)]
+        banks = {(m, q): psum.tile([P, QUARTER], F32, name=f"bank{m}{q}") for m, q in order}
+
+        def multiply(t, o):
+            for m, q in order:
+                first = t * S + q * QUARTER
+                nc.tensor.matmul_mx(
+                    out=banks[m, q][:],
+                    lhsT=codes[t, o][:, m * P : (m + 1) * P].bitcast(FP8X4),
+                    lhsT_scale=scales[t, o][:, m * P : (m + 1) * P],
+                    rhs=picked[t, o, q].bitcast(FP8X4),
+                    rhs_scale=planes[ROWS * o :, first : first + QUARTER],
+                    start=(t, o) == (X, 0),
+                    stop=(t, o) == (E, 1),
+                )
+
+        pick(X, 0, 1)
+        pick(X, 1, 1)
+        pick(E, 0, 1)
+        pick(E, 1, QUARTERS)
+        for t in (X, E):
+            for o in range(PASSES):
+                multiply(t, o)
+
+        stores = [(0, 0, 1), (1, 0, 2), (0, 1, 2), (1, 2, 2), (0, 3, 1)]
+        results = {}
+        for m, first, count in stores:
+            results[m, first] = tile([P, count * QUARTER], F32, f"result{m}{first}")
+        for m, q in order:
+            for sm, first, count in stores:
+                if sm == m and first <= q < first + count:
+                    result = results[m, first]
+                    nc.scalar.activation(result[:, (q - first) * QUARTER : (q - first + 1) * QUARTER], banks[m, q][:], SIGMOID)
+                    if q == first + count - 1:
+                        nc.sync.dma_start(out=out[m * P : (m + 1) * P, first * QUARTER : (first + count) * QUARTER], in_=result[:])

@@ -129,8 +129,8 @@ def tile_picked_zhyb_sig_p_kernel(tc, x_words, x_scales, e_words, e_scales, hT, 
         order = [(0, 0), (1, 0), (1, 1), (0, 1), (0, 2), (1, 2), (1, 3), (0, 3)]
         banks = {(m, q): psum.tile([P, QUARTER], F32, name=f"bank{m}{q}") for m, q in order}
 
-        def multiply(t, o):
-            for m, q in order:
+        def multiply(t, o, pieces):
+            for m, q in pieces:
                 first = t * S + q * QUARTER
                 nc.tensor.matmul_mx(
                     out=banks[m, q][:],
@@ -144,11 +144,14 @@ def tile_picked_zhyb_sig_p_kernel(tc, x_words, x_scales, e_words, e_scales, hT, 
 
         pick(X, 0, 1)
         pick(X, 1, 1)
-        pick(E, 0, 1)
+        pick(E, 0, 2)
         pick(E, 1, QUARTERS)
-        for t in (X, E):
-            for o in range(PASSES):
-                multiply(t, o)
+        half = len(order) // 2
+        multiply(X, 0, order)
+        multiply(X, 1, order[:half])
+        multiply(E, 0, order)
+        multiply(X, 1, order[half:])
+        multiply(E, 1, order)
 
         stores = [(0, 0, 1), (1, 0, 2), (0, 1, 2), (1, 2, 2), (0, 3, 1)]
         results = {}

@@ -67,6 +67,7 @@ def tile_picked_zhyb_sig_p_kernel(tc, x_words, x_scales, e_words, e_scales, hT, 
             nc.sync.dma_start(
                 out=words[t, o][:].bitcast(I32),
                 in_=words_in[t][o].rearrange("p n r -> p (n r)").bitcast(I32),
+                max_dma_last_dim=4096,
             )
 
         load_queries(X, 0)

@@ -45,9 +45,9 @@ def tile_picked_zhyb_sig_p_kernel(tc, x_words, x_scales, e_words, e_scales, hT, 
 
         raw = {}
 
-        def load_queries(t, o):
-            raw[t, o] = tile([P, PACK * J], F32, f"raw{t}{o}")
-            nc.sync.dma_start(out=raw[t, o][:], in_=queries_in[t].rearrange("(o p r) j -> o p (r j)", o=PASSES, r=PACK)[o])
+        def load_queries(t, o, queue, tag=None):
+            raw[t, o] = tile([P, PACK * J], F32, f"raw{t}{o}", tag)
+            queue.dma_start(out=raw[t, o][:], in_=queries_in[t].rearrange("(o p r) j -> o p (r j)", o=PASSES, r=PACK)[o])
 
         scale_rows = {}
 
@@ -62,23 +62,21 @@ def tile_picked_zhyb_sig_p_kernel(tc, x_words, x_scales, e_words, e_scales, hT, 
 
         words = {}
 
-        def load_words(t, o, tag=None):
+        def load_words(t, o, queue, tag=None):
             words[t, o] = tile([P, T], U32, f"words{t}{o}", tag)
-            nc.sync.dma_start(
+            queue.dma_start(
                 out=words[t, o][:].bitcast(I32),
                 in_=words_in[t][o].rearrange("p n r -> p (n r)").bitcast(I32),
                 max_dma_last_dim=4096,
             )
 
-        load_queries(X, 0)
+        load_queries(X, 0, nc.sync)
         nc.sync.dma_start(offsets[:], offs)
         load_scale_rows(X)
-        load_queries(E, 0)
+        load_queries(E, 0, nc.sync)
         load_scale_rows(E)
-        load_queries(X, 1)
-        load_queries(E, 1)
-        load_words(X, 0)
-        load_words(X, 1)
+        load_queries(X, 1, nc.sync)
+        load_words(X, 0, nc.sync)
 
         picked_scales = tile([P, 2 * S], U8, "picked_scales")
         for t in (X, E):
@@ -95,6 +93,7 @@ def tile_picked_zhyb_sig_p_kernel(tc, x_words, x_scales, e_words, e_scales, hT, 
 
         codes = {}
         scales = {}
+        query_scales = tile([P, 2 * PASSES * J], U8, "query_scales", f"scale_rows{E}")
 
         def quantise(t, o):
             grouped = tile([P, J, PACK], BF16, f"grouped{t}{o}")
@@ -103,18 +102,21 @@ def tile_picked_zhyb_sig_p_kernel(tc, x_words, x_scales, e_words, e_scales, hT, 
                 in_=raw[t, o][:].rearrange("p (r c i) -> p c r i", r=PACK, i=4),
             )
             codes[t, o] = tile([P, J], U32, f"codes{t}{o}")
-            scales[t, o] = tile([P, J], U8, f"scales{t}{o}")
+            scales[t, o] = query_scales[:, (PASSES * t + o) * J : (PASSES * t + o + 1) * J]
             nc.vector.quantize_mx(
                 out=codes[t, o][:].bitcast(FP8X4),
-                scales=scales[t, o][:],
+                scales=scales[t, o],
                 in_=grouped[:].rearrange("p j r -> p (j r)"),
             )
 
-        for o in range(PASSES):
-            for t in (X, E):
-                quantise(t, o)
-        load_words(E, 0, "grouped10")
-        load_words(E, 1, "grouped11")
+        quantise(X, 0)
+        load_queries(E, 1, nc.scalar, "raw00")
+        quantise(E, 0)
+        load_words(X, 1, nc.scalar, "raw10")
+        quantise(X, 1)
+        quantise(E, 1)
+        load_words(E, 0, nc.sync, "grouped10")
+        load_words(E, 1, nc.sync, "grouped01")
 
         picked = {}
 

@@ -84,8 +84,8 @@ def tile_picked_zhyb_sig_p_kernel(tc, x_words, x_scales, e_words, e_scales, hT, 
 
         planes = tile([P, 2 * S], U8, "planes")
         nc.vector.tensor_copy(planes[:].bitcast(I32), picked_scales[:].bitcast(I32))
-        for o in range(PASSES):
-            for i in range(1, ROWS):
+        for i in range(1, ROWS):
+            for o in range(PASSES):
                 nc.sync.dma_start(
                     out=planes[ROWS * o + i : P : QUAD, :].bitcast(I32),
                     in_=picked_scales[ROWS * o + SPREAD * i : P : QUAD, :].bitcast(I32),

@@ -37,7 +37,7 @@ def tile_picked_zhyb_sig_p_kernel(tc, x_words, x_scales, e_words, e_scales, hT, 
         def tile(shape, dtype, name, tag=None):
             return keep.tile(shape, dtype, name=name, tag=tag or name, align_bytes=ALIGN)
 
-        offsets = keep.tile([P, S // STRIPE], U16, name="offsets")
+        offsets = tile([P, S // STRIPE], U16, "offsets")
 
         words_in = {X: x_words, E: e_words}
         scales_in = {X: x_scales, E: e_scales}

from contextlib import ExitStack

import concourse.mybir as mybir

K, T, S, J = 1024, 2048, 512, 256
FLOPS = 2 * 2 * K * J * S

F32 = mybir.dt.float32
BF16 = mybir.dt.bfloat16
I32 = mybir.dt.int32
U32 = mybir.dt.uint32
U16 = mybir.dt.uint16
U8 = mybir.dt.uint8
FP8X4 = mybir.dt.float8_e4m3fn_x4
SIGMOID = mybir.ActivationFunctionType.Sigmoid

P = 128
PACK = 4
K_PASS = P * PACK
PASSES = K // K_PASS
QUARTERS = 4
QUARTER = S // QUARTERS
STRIPE = 16
QUAD = 32
ROWS = 4
SPREAD = 8
ALIGN = 512
X, E = 0, 1


def tile_picked_zhyb_sig_p_kernel(tc, x_words, x_scales, e_words, e_scales, hT, gT, offs, out):
    nc = tc.nc
    with ExitStack() as ctx:
        keep = ctx.enter_context(tc.tile_pool(name="keep", bufs=1))
        psum = ctx.enter_context(tc.psum_pool(name="psum", bufs=1))

        def tile(shape, dtype, name, tag=None):
            return keep.tile(shape, dtype, name=name, tag=tag or name, align_bytes=ALIGN)

        offsets = tile([P, S // STRIPE], U16, "offsets")

        words_in = {X: x_words, E: e_words}
        scales_in = {X: x_scales, E: e_scales}
        queries_in = {X: hT, E: gT}

        raw = {}

        def load_queries(t, o, queue, tag=None):
            raw[t, o] = tile([P, PACK * J], F32, f"raw{t}{o}", tag)
            queue.dma_start(out=raw[t, o][:], in_=queries_in[t].rearrange("(o p r) j -> o p (r j)", o=PASSES, r=PACK)[o])

        scale_rows = {}

        def load_scale_rows(t):
            scale_rows[t] = tile([P, T], U8, f"scale_rows{t}")
            nc.vector.memset(scale_rows[t][:].bitcast(I32), 0)
            for o in range(PASSES):
                nc.sync.dma_start(
                    out=scale_rows[t][ROWS * o : P : SPREAD, :].bitcast(I32),
                    in_=scales_in[t][o].bitcast(I32),
                )

        words = {}

        def load_words(t, o, queue, tag=None):
            words[t, o] = tile([P, T], U32, f"words{t}{o}", tag)
            queue.dma_start(
                out=words[t, o][:].bitcast(I32),
                in_=words_in[t][o].rearrange("p n r -> p (n r)").bitcast(I32),
                max_dma_last_dim=4096,
            )

        load_queries(X, 0, nc.sync)
        nc.sync.dma_start(offsets[:], offs)
        load_scale_rows(X)
        load_queries(E, 0, nc.sync)
        load_scale_rows(E)
        load_queries(X, 1, nc.sync)
        load_words(X, 0, nc.sync)

        picked_scales = tile([P, 2 * S], U8, "picked_scales")
        for t in (X, E):
            nc.vector.tensor_copy(picked_scales[:, t * S : (t + 1) * S], scale_rows[t][:].indirect(offsets[:]))

        planes = tile([P, 2 * S], U8, "planes")
        nc.vector.tensor_copy(planes[:].bitcast(I32), picked_scales[:].bitcast(I32))
        for i in range(1, ROWS):
            for o in range(PASSES):
                nc.sync.dma_start(
                    out=planes[ROWS * o + i : P : QUAD, :].bitcast(I32),
                    in_=picked_scales[ROWS * o + SPREAD * i : P : QUAD, :].bitcast(I32),
                )

        codes = {}
        scales = {}
        query_scales = tile([P, 2 * PASSES * J], U8, "query_scales", f"scale_rows{E}")

        def quantise(t, o):
            grouped = tile([P, J, PACK], BF16, f"grouped{t}{o}")
            nc.scalar.copy(
                out=grouped[:].rearrange("p (c i) r -> p c r i", i=4),
                in_=raw[t, o][:].rearrange("p (r c i) -> p c r i", r=PACK, i=4),
            )
            codes[t, o] = tile([P, J], U32, f"codes{t}{o}")
            scales[t, o] = query_scales[:, (PASSES * t + o) * J : (PASSES * t + o + 1) * J]
            nc.vector.quantize_mx(
                out=codes[t, o][:].bitcast(FP8X4),
                scales=scales[t, o],
                in_=grouped[:].rearrange("p j r -> p (j r)"),
            )

        quantise(X, 0)
        load_queries(E, 1, nc.scalar, "raw00")
        quantise(E, 0)
        load_words(X, 1, nc.scalar, "raw10")
        quantise(X, 1)
        quantise(E, 1)
        load_words(E, 0, nc.sync, "grouped10")
        load_words(E, 1, nc.sync, "grouped01")

        picked = {}

        def pick(t, o, parts):
            width = S // parts
            for part in range(parts):
                one = tile([P, width], U32, f"picked{t}{o}{part}")
                columns = slice(part * width // STRIPE, (part + 1) * width // STRIPE)
                nc.vector.tensor_copy(one[:], words[t, o][:].indirect(offsets[:, columns]))
                for n in range(width // QUARTER):
                    picked[t, o, part * width // QUARTER + n] = one[:, n * QUARTER : (n + 1) * QUARTER]

        order = [(0, 0), (1, 0), (1, 1), (0, 1), (0, 2), (1, 2), (1, 3), (0, 3)]
        banks = {(m, q): psum.tile([P, QUARTER], F32, name=f"bank{m}{q}") for m, q in order}

        def multiply(t, o, pieces):
            for m, q in pieces:
                first = t * S + q * QUARTER
                nc.tensor.matmul_mx(
                    out=banks[m, q][:],
                    lhsT=codes[t, o][:, m * P : (m + 1) * P].bitcast(FP8X4),
                    lhsT_scale=scales[t, o][:, m * P : (m + 1) * P],
                    rhs=picked[t, o, q].bitcast(FP8X4),
                    rhs_scale=planes[ROWS * o :, first : first + QUARTER],
                    start=(t, o) == (X, 0),
                    stop=(t, o) == (E, 1),
                )

        pick(X, 0, 1)
        pick(X, 1, 1)
        pick(E, 0, 2)
        pick(E, 1, QUARTERS)
        half = len(order) // 2
        multiply(X, 0, order)
        multiply(X, 1, order[:half])
        multiply(E, 0, order)
        multiply(X, 1, order[half:])
        multiply(E, 1, order)

        stores = [(0, 0, 1), (1, 0, 2), (0, 1, 2), (1, 2, 2), (0, 3, 1)]
        results = {}
        for m, first, count in stores:
            results[m, first] = tile([P, count * QUARTER], F32, f"result{m}{first}")
        for m, q in order:
            for sm, first, count in stores:
                if sm == m and first <= q < first + count:
                    result = results[m, first]
                    nc.scalar.activation(result[:, (q - first) * QUARTER : (q - first + 1) * QUARTER], banks[m, q][:], SIGMOID)
                    if q == first + count - 1:
                        nc.sync.dma_start(out=out[m * P : (m + 1) * P, first * QUARTER : (first + count) * QUARTER], in_=result[:])
